import numpy as np
import ml_dtypes


def mxq(x, axis, fmt="e4m3"):
    dtype, down = {"e4m3": (ml_dtypes.float8_e4m3fn, 7), "e5m2": (ml_dtypes.float8_e5m2, 14)}[fmt]
    v = np.moveaxis(np.asarray(x, np.float32).astype(ml_dtypes.bfloat16).astype(np.float64), axis, -1)
    blocks = v.reshape(v.shape[:-1] + (-1, 32))
    amax = np.abs(blocks).max(-1, keepdims=True)
    byte = np.maximum(np.where(amax > 0, np.frexp(amax)[1] - 1 + 127, 0) - down, 1)
    scale = np.exp2(byte - 127.0)
    codes = (blocks / scale).astype(np.float32).astype(dtype).astype(np.float64)
    return np.moveaxis((codes * scale).reshape(v.shape), -1, axis)


WIDE = False


def mx_kscale(k):
    if not WIDE:
        return np.ones(k)
    levels = np.array([10, -10, 5, -5, 0])
    if k % 512:
        return np.exp2(np.random.permutation(np.resize(levels, k // 32))).repeat(32)
    a = np.empty((k // 512, 16))
    for p in range(k // 512):
        a[p, :8] = np.random.permutation(np.resize(levels, 8))
        for g in range(8):
            far = levels[np.abs(levels - a[p, g]) >= 10]
            a[p, g + 8] = far[np.random.randint(len(far))]
    return np.exp2(a.ravel()).repeat(32)


def f64(x):
    return np.asarray(x).astype(np.float64)


def striped(idx):
    return np.tile(idx.reshape(-1, 16).T, (8, 1)).astype(np.uint16)


def unstriped(offs):
    return offs[:16].T.reshape(-1).astype(np.int64)


E2M1 = np.array([0.0, 0.5, 1.0, 1.5, 2.0, 3.0, 4.0, 6.0, -0.0, -0.5, -1.0, -1.5, -2.0, -3.0, -4.0, -6.0])


def pack_weight(w, fmt):
    k, n = w.shape
    w = f64(np.asarray(w, np.float32).astype(ml_dtypes.bfloat16)).reshape(k // 32, 32, n)
    amax = np.abs(w).max(1)
    if fmt == "e4m3":
        byte = np.frexp(amax)[1] - 1 + 127 - 7
    else:
        mant, ex = np.frexp(amax / 6.0)
        byte = np.where(mant > 0.5, ex, ex - 1) + 127
    byte = np.clip(np.where(amax > 0, byte, 1), 1, 254)
    scaled = (w * np.exp2(127.0 - byte)[:, None, :]).reshape(k, n).astype(np.float32)
    by_word = np.ascontiguousarray(scaled.reshape(k // 512, 128, 4, n).transpose(0, 1, 3, 2))
    if fmt == "e4m3":
        words = by_word.astype(ml_dtypes.float8_e4m3fn).view(np.uint8)
    else:
        c = by_word.astype(ml_dtypes.float4_e2m1fn).view(np.uint8) & 0xF
        words = (c[..., 0::2] | (c[..., 1::2] << 4)).reshape(k // 512, 128, 2 * n)
    return np.ascontiguousarray(words), np.ascontiguousarray(byte.astype(np.uint8).reshape(k // 512, 16, n))


def unpack_weight(words, scales, fmt):
    g, _, n = scales.shape
    words = np.ascontiguousarray(words).reshape(g, 128, n, -1)
    if fmt == "e4m3":
        vals = words.view(ml_dtypes.float8_e4m3fn).astype(np.float64)
    else:
        nib = np.empty((g, 128, n, 4), np.uint8)
        nib[..., 0::2] = words & 0xF
        nib[..., 1::2] = words >> 4
        vals = E2M1[nib]
    vals = vals * np.repeat(np.exp2(scales.astype(np.float64) - 127.0), 8, axis=1)[..., None]
    return vals.transpose(0, 1, 3, 2).reshape(g * 512, n)


def gelu(v):
    return 0.5 * v * (1.0 + np.tanh(np.sqrt(2.0 / np.pi) * (v + 0.044715 * v**3)))


def often(T, S):
    return np.random.permutation(T)[(T * np.random.uniform(0, 1, S) ** 4).astype(np.int64)]


K, M, H, T, S, P = 1024, 512, 1024, 2048, 1024, 512


def setup_inputs():
    n = np.random.standard_normal
    s, s2, u = mx_kscale(K)[:, None], mx_kscale(M)[:, None], mx_kscale(H)[:, None]
    d = {}
    d["tab_words"], d["tab_scales"] = pack_weight(n((K, T)) * s, "e4m3")
    d["tab2_words"], d["tab2_scales"] = pack_weight(n((M, T)) * s2, "e4m3")
    d["tab3_words"], d["tab3_scales"] = pack_weight(n((M, T)) * s2, "e4m3")
    d["offs"] = striped(np.random.permutation(T)[:S])
    d["offs2"] = striped(np.random.permutation(T)[:S])
    d["offs3"] = striped(np.random.permutation(T)[:S])
    d["pos1"] = striped(np.random.permutation(S)[:P])
    d["pos2"] = striped(often(S, P))
    d["pos3"] = striped(often(S, P))
    d["w1"] = (n((K, H)) / K**0.5 / s * u.T).astype(np.float32)
    d["w2_words"], d["w2_scales"] = pack_weight(n((M, H)) / M**0.5 / s2 * u.T, "e2m1")
    d["w3"] = (n((M, H)) / M**0.5 / s2 * u.T).astype(np.float32)
    d["w4_words"], d["w4_scales"] = pack_weight(n((H, H)) / H**0.5 / u, "e4m3")
    d["gd"] = (0.9 * np.exp(0.3 * n(H)) / u[:, 0]).astype(np.float32)
    return d


def reference(tab_words, tab_scales, tab2_words, tab2_scales, tab3_words, tab3_scales, offs, offs2, offs3,
              pos1, pos2, pos3, w1, w2_words, w2_scales, w3, w4_words, w4_scales, gd):
    v = unpack_weight(tab_words, tab_scales, "e4m3")[:, unstriped(offs)]
    v2 = unpack_weight(tab2_words, tab2_scales, "e4m3")[:, unstriped(offs2)]
    v3 = unpack_weight(tab3_words, tab3_scales, "e4m3")[:, unstriped(offs3)]
    a = mxq(f64(w1), 0, "e4m3").T @ v
    b = unpack_weight(w2_words, w2_scales, "e2m1").T @ v2
    d = mxq(f64(w3), 0, "e4m3").T @ v3
    dp = d[:, unstriped(pos3)]
    z = np.maximum(a[:, unstriped(pos1)], b[:, unstriped(pos2)]) - np.abs(dp)
    y = unpack_weight(w4_words, w4_scales, "e4m3").T @ mxq(z, 0, "e4m3")
    return np.tanh(y + f64(gd)[:, None] * dp)

@@ -1,0 +1,244 @@
+from contextlib import ExitStack
+
+import concourse.mybir as mybir
+
+K, M, H, T, S, J = 1024, 512, 1024, 2048, 1024, 512
+FLOPS = 2 * H * S * (K + M + M) + 2 * H * H * J
+
+F32 = mybir.dt.float32
+BF16 = mybir.dt.bfloat16
+I32 = mybir.dt.int32
+U32 = mybir.dt.uint32
+U16 = mybir.dt.uint16
+U8 = mybir.dt.uint8
+FP8X4 = mybir.dt.float8_e4m3fn_x4
+FP4X4 = mybir.dt.float4_e2m1fn_x4
+ALU = mybir.AluOpType
+ACT = mybir.ActivationFunctionType
+
+P = 128
+PACK = 4
+K_PASS = P * PACK
+N_BANK = 512
+QUADS = 4
+HALVES = H // K_PASS
+
+
+def tile_list_carton_seal_join_kernel(
+    tc, tab_words, tab_scales, tab2_words, tab2_scales, tab3_words, tab3_scales, offs, offs2, offs3,
+    pos1, pos2, pos3, w1, w2_words, w2_scales, w3, w4_words, w4_scales, gd, out,
+):
+    nc = tc.nc
+    with ExitStack() as ctx:
+        keep = ctx.enter_context(tc.tile_pool(name="keep", bufs=1))
+        ring = ctx.enter_context(tc.tile_pool(name="ring", bufs=1))
+        psum = ctx.enter_context(tc.psum_pool(name="psum", bufs=8))
+
+        def load_list(src, name):
+            tile = keep.tile(list(src.shape), U16, name=name)
+            nc.sync.dma_start(tile[:], src)
+            return tile
+
+        def load_words(src, name):
+            tile = keep.tile([P, T], I32, name=name, align_bytes=64)
+            nc.sync.dma_start(tile[:], src.rearrange("p t i -> p (t i)").bitcast(I32))
+            return tile
+
+        def zeroed_plane(width, name, engine):
+            tile = keep.tile([P, width], U8, name=name, align_bytes=64)
+            engine.memset(tile[:].bitcast(I32), 0)
+            return tile
+
+        def load_scale_rows(plane, src, first_row):
+            rows = 4 * src.shape[0]
+            for quad in range(QUADS):
+                lo = 32 * quad + first_row
+                nc.sync.dma_start(plane[lo : lo + rows, :].bitcast(I32), src[:, 4 * quad : 4 * quad + 4, :].bitcast(I32))
+
+        def load_weight(src, a, b):
+            raw = ring.tile([P, PACK, K_PASS], F32, name="raw", tag="raw", bufs=4, align_bytes=64)
+            rows = src[K_PASS * a : K_PASS * (a + 1), K_PASS * b : K_PASS * (b + 1)]
+            nc.sync.dma_start(raw[:], rows.rearrange("(p j) c -> p j c", j=PACK))
+            return raw
+
+        def gather_words(table, offsets, name):
+            picked = keep.tile([P, S], U32, name=name, align_bytes=64)
+            nc.vector.tensor_copy(picked[:], table[:].bitcast(U32).indirect(offsets[:]))
+            return picked
+
+        def gather_scales(plane, offsets, name):
+            picked = keep.tile([P, S], U8, name=name, align_bytes=64)
+            nc.vector.tensor_copy(picked[:], plane[:].indirect(offsets[:]))
+            return picked
+
+        def cast_weight(raw):
+            grouped = ring.tile([P, PACK * K_PASS], BF16, name="grouped", tag="grouped", bufs=3, align_bytes=64)
+            nc.scalar.copy(
+                grouped[:].rearrange("p (t q j) -> p q t j", t=PACK, j=PACK),
+                raw[:].rearrange("p j (q t) -> p q t j", t=PACK),
+            )
+            return grouped
+
+        def quantize(grouped, name):
+            codes = keep.tile([P, K_PASS], U32, name=name + "_codes", align_bytes=64)
+            scales = keep.tile([P, K_PASS], U8, name=name + "_scales", align_bytes=64)
+            nc.vector.quantize_mx(out=codes[:].bitcast(FP8X4), scales=scales[:], in_=grouped[:])
+            return codes, scales
+
+        def first_stage(passes):
+            window = ring.tile([P, S], F32, name="window", tag="window", bufs=10, align_bytes=64)
+            for h in range(S // N_BANK):
+                cols = slice(h * N_BANK, (h + 1) * N_BANK)
+                acc = psum.tile([P, N_BANK], F32, name="acc", tag="acc")
+                for i, (lhs, lhs_scale, words, plane, row) in enumerate(passes):
+                    nc.tensor.matmul_mx(
+                        out=acc[:], lhsT=lhs, lhsT_scale=lhs_scale,
+                        rhs=words[:, cols].bitcast(FP8X4), rhs_scale=plane[row:P, cols],
+                        start=(i == 0), stop=(i == len(passes) - 1),
+                    )
+                nc.scalar.copy(window[:, cols], acc[:])
+            return window
+
+        tab3_plane = zeroed_plane(T, "tab3_plane", nc.vector)
+        tab2_plane = zeroed_plane(T, "tab2_plane", nc.gpsimd)
+        w_plane = zeroed_plane(H, "w_plane", nc.vector)
+        tab_plane = zeroed_plane(T, "tab_plane", nc.vector)
+
+        l_offs3 = load_list(offs3, "l_offs3")
+        t3 = load_words(tab3_words[0], "t3")
+        load_scale_rows(tab3_plane, tab3_scales, 0)
+        w3_raw = [load_weight(w3, 0, 0)]
+        l_offs2 = load_list(offs2, "l_offs2")
+        t2 = load_words(tab2_words[0], "t2")
+        load_scale_rows(tab2_plane, tab2_scales, 0)
+        w3_raw.append(load_weight(w3, 0, 1))
+        w2_raw = keep.tile([P, 2 * H], U8, name="w2_raw", align_bytes=64)
+        nc.sync.dma_start(w2_raw[:].bitcast(I32), w2_words[0].bitcast(I32))
+        load_scale_rows(w_plane, w2_scales, 0)
+        l_offs = load_list(offs, "l_offs")
+        t1 = [load_words(tab_words[0], "t1a")]
+        load_scale_rows(w_plane, w4_scales, 4)
+        l_pos3 = load_list(pos3, "l_pos3")
+        t1.append(load_words(tab_words[1], "t1b"))
+        load_scale_rows(tab_plane, tab_scales, 0)
+        l_pos2 = load_list(pos2, "l_pos2")
+        l_pos1 = load_list(pos1, "l_pos1")
+        w1_raw = {}
+        for b in range(HALVES):
+            for a in range(K // K_PASS):
+                w1_raw[a, b] = load_weight(w1, a, b)
+        gain = keep.tile([P, HALVES, PACK], F32, name="gain")
+        nc.sync.dma_start(gain[:], gd.rearrange("(b p t) -> p b t", p=P, t=PACK))
+        w4_raw = keep.tile([P, 2, H], I32, name="w4_raw", align_bytes=64)
+        nc.sync.dma_start(w4_raw[:], w4_words.rearrange("a p c i -> p a (c i)").bitcast(I32))
+
+        v3 = gather_words(t3, l_offs3, "v3")
+        v3_plane = gather_scales(tab3_plane, l_offs3, "v3_plane")
+        w3_q = [quantize(cast_weight(w3_raw[0]), "w3_0")]
+        v2 = gather_words(t2, l_offs2, "v2")
+        v2_plane = gather_scales(tab2_plane, l_offs2, "v2_plane")
+        w3_q.append(quantize(cast_weight(w3_raw[1]), "w3_1"))
+
+        w2_dealt = keep.tile([P, 2 * H], U8, name="w2_dealt", align_bytes=64)
+        w_plane_dealt = keep.tile([P, H], U8, name="w_plane_dealt", align_bytes=64)
+        for b in range(HALVES):
+            cols = slice(K_PASS * b, K_PASS * (b + 1))
+            two = slice(2 * K_PASS * b, 2 * K_PASS * (b + 1))
+            nc.gpsimd.tensor_copy(
+                w2_dealt[:, two].rearrange("p (t q e) -> p t q e", t=PACK, e=2),
+                w2_raw[:, two].rearrange("p (q t e) -> p t q e", t=PACK, e=2),
+            )
+            nc.gpsimd.tensor_copy(
+                w_plane_dealt[:, cols].rearrange("p (t q) -> p t q", t=PACK),
+                w_plane[:, cols].rearrange("p (q t) -> p t q", t=PACK),
+            )
+
+        v1 = [gather_words(t1[0], l_offs, "v1a"), gather_words(t1[1], l_offs, "v1b")]
+        v1_plane = gather_scales(tab_plane, l_offs, "v1_plane")
+
+        d_picked = [keep.tile([P, PACK, J], F32, name="d_picked%d" % b, align_bytes=64) for b in range(HALVES)]
+        best = [keep.tile([P, PACK, J], F32, name="best%d" % b, align_bytes=64) for b in range(HALVES)]
+
+        def slice_d(b, t):
+            cols = slice(P * t, P * (t + 1))
+            codes, scales = w3_q[b]
+            window = first_stage([(codes[:, cols].bitcast(FP8X4), scales[:, cols], v3, v3_plane, 0)])
+            nc.vector.tensor_copy(d_picked[b][:, t, :], window[:].indirect(l_pos3[:]))
+
+        def slice_b(b, t):
+            lo = K_PASS * b + P * t
+            window = first_stage([(w2_dealt[:, 2 * lo : 2 * (lo + P)].bitcast(FP4X4), w_plane_dealt[:, lo : lo + P], v2, v2_plane, 0)])
+            nc.vector.tensor_copy(best[b][:, t, :], window[:].indirect(l_pos2[:]))
+
+        w1_q = {}
+
+        def slice_a(b, t):
+            cols = slice(P * t, P * (t + 1))
+            window = first_stage([
+                (w1_q[a, b][0][:, cols].bitcast(FP8X4), w1_q[a, b][1][:, cols], v1[a], v1_plane, 4 * a)
+                for a in range(K // K_PASS)
+            ])
+            a_picked = ring.tile([P, J], F32, name="a_picked", tag="a_picked", bufs=2, align_bytes=64)
+            nc.vector.tensor_copy(a_picked[:], window[:].indirect(l_pos1[:]))
+            nc.vector.tensor_tensor(best[b][:, t, :], a_picked[:], best[b][:, t, :], ALU.max)
+
+        def join(b):
+            d_abs = ring.tile([P, PACK, J], F32, name="d_abs", tag="raw", bufs=4, align_bytes=64)
+            nc.scalar.activation(d_abs[:], d_picked[b][:], ACT.Abs)
+            grouped = ring.tile([P, PACK * J], BF16, name="grouped", tag="grouped", bufs=3, align_bytes=64)
+            nc.vector.tensor_tensor(
+                grouped[:].rearrange("p (c i t) -> p c t i", i=4, t=PACK),
+                best[b][:].rearrange("p t (c i) -> p c t i", i=4),
+                d_abs[:].rearrange("p t (c i) -> p c t i", i=4),
+                ALU.subtract,
+            )
+            return quantize(grouped, "z%d" % b)
+
+        for t in range(PACK):
+            slice_d(0, t)
+        for t in range(PACK):
+            slice_b(0, t)
+        for a in range(K // K_PASS):
+            w1_q[a, 0] = quantize(cast_weight(w1_raw[a, 0]), "w1_%d0" % a)
+        for t in range(PACK):
+            slice_d(1, t)
+        for a in range(K // K_PASS):
+            w1_q[a, 1] = quantize(cast_weight(w1_raw[a, 1]), "w1_%d1" % a)
+        for t in range(PACK):
+            slice_b(1, t)
+        for t in range(PACK):
+            slice_a(0, t)
+        z_q = [join(0)]
+
+        w4_dealt = keep.tile([P, 2, H], I32, name="w4_dealt", align_bytes=64)
+        for a in range(HALVES):
+            for b in range(HALVES):
+                cols = slice(K_PASS * b, K_PASS * (b + 1))
+                nc.gpsimd.tensor_copy(
+                    w4_dealt[:, a, cols].rearrange("p (t q) -> p t q", t=PACK),
+                    w4_raw[:, a, cols].rearrange("p (q t) -> p t q", t=PACK),
+                )
+
+        for t in range(PACK):
+            slice_a(1, t)
+        z_q.append(join(1))
+
+        out_rows = out.rearrange("(b p t) j -> b p t j", p=P, t=PACK)
+        for b in range(HALVES):
+            result = ring.tile([P, PACK, J], F32, name="result", tag="raw", bufs=4, align_bytes=64)
+            for t in range(PACK):
+                lo = K_PASS * b + P * t
+                acc = psum.tile([P, J], F32, name="acc", tag="acc")
+                for a in range(HALVES):
+                    nc.tensor.matmul_mx(
+                        out=acc[:], lhsT=w4_dealt[:, a, lo : lo + P].bitcast(FP8X4),
+                        lhsT_scale=w_plane_dealt[4 + 4 * a : P, lo : lo + P],
+                        rhs=z_q[a][0][:].bitcast(FP8X4), rhs_scale=z_q[a][1][:],
+                        start=(a == 0), stop=(a == HALVES - 1),
+                    )
+                summed = ring.tile([P, J], F32, name="summed", tag="a_picked", bufs=2, align_bytes=64)
+                nc.vector.scalar_tensor_tensor(
+                    summed[:], d_picked[b][:, t, :], gain[:, b, t : t + 1], acc[:], ALU.mult, ALU.add
+                )
+                nc.scalar.activation(result[:, t, :], summed[:], ACT.Tanh)
+                nc.sync.dma_start(out_rows[b, :, t, :], result[:, t, :])

@@ -71,22 +71,25 @@ def tile_list_carton_seal_join_kernel(
             nc.vector.tensor_copy(picked[:], plane[:].indirect(offsets[:]))
             return picked
 
-        def cast_weight(raw):
-            grouped = ring.tile([P, PACK * K_PASS], BF16, name="grouped", tag="grouped", bufs=3, align_bytes=64)
-            nc.scalar.copy(
-                grouped[:].rearrange("p (t q j) -> p q t j", t=PACK, j=PACK),
-                raw[:].rearrange("p j (q t) -> p q t j", t=PACK),
-            )
+        def cast_weight(raw, on_scalar):
+            grouped = ring.tile([P, PACK * K_PASS], BF16, name="grouped", tag="grouped", bufs=5, align_bytes=64)
+            dst = grouped[:].rearrange("p (t q j) -> p q t j", t=PACK, j=PACK)
+            src = raw[:].rearrange("p j (q t) -> p q t j", t=PACK)
+            if on_scalar:
+                nc.scalar.copy(dst, src)
+            else:
+                nc.gpsimd.tensor_scalar(dst, src, 1.0, 0.0, ALU.mult, ALU.add)
             return grouped
 
         def quantize(grouped, name):
-            codes = keep.tile([P, K_PASS], U32, name=name + "_codes", align_bytes=64)
-            scales = keep.tile([P, K_PASS], U8, name=name + "_scales", align_bytes=64)
+            width = grouped.shape[1] // PACK
+            codes = keep.tile([P, width], U32, name=name + "_codes", align_bytes=64)
+            scales = keep.tile([P, width], U8, name=name + "_scales", align_bytes=64)
             nc.vector.quantize_mx(out=codes[:].bitcast(FP8X4), scales=scales[:], in_=grouped[:])
             return codes, scales
 
         def first_stage(passes):
-            window = ring.tile([P, S], F32, name="window", tag="window", bufs=10, align_bytes=64)
+            window = ring.tile([P, S], F32, name="window", tag="window", bufs=8, align_bytes=64)
             for h in range(S // N_BANK):
                 cols = slice(h * N_BANK, (h + 1) * N_BANK)
                 acc = psum.tile([P, N_BANK], F32, name="acc", tag="acc")
@@ -99,62 +102,66 @@ def tile_list_carton_seal_join_kernel(
                 nc.scalar.copy(window[:, cols], acc[:])
             return window
 
-        tab3_plane = zeroed_plane(T, "tab3_plane", nc.vector)
         tab2_plane = zeroed_plane(T, "tab2_plane", nc.gpsimd)
-        w_plane = zeroed_plane(H, "w_plane", nc.vector)
+        w2_plane = zeroed_plane(H, "w2_plane", nc.vector)
+        tab3_plane = zeroed_plane(T, "tab3_plane", nc.vector)
         tab_plane = zeroed_plane(T, "tab_plane", nc.vector)
+        w4_plane = zeroed_plane(H, "w4_plane", nc.gpsimd)
 
-        l_offs3 = load_list(offs3, "l_offs3")
-        t3 = load_words(tab3_words[0], "t3")
-        load_scale_rows(tab3_plane, tab3_scales, 0)
-        w3_raw = [load_weight(w3, 0, 0)]
         l_offs2 = load_list(offs2, "l_offs2")
-        t2 = load_words(tab2_words[0], "t2")
         load_scale_rows(tab2_plane, tab2_scales, 0)
-        w3_raw.append(load_weight(w3, 0, 1))
+        t2 = load_words(tab2_words[0], "t2")
         w2_raw = keep.tile([P, 2 * H], U8, name="w2_raw", align_bytes=64)
         nc.sync.dma_start(w2_raw[:].bitcast(I32), w2_words[0].bitcast(I32))
-        load_scale_rows(w_plane, w2_scales, 0)
-        l_offs = load_list(offs, "l_offs")
-        t1 = [load_words(tab_words[0], "t1a")]
-        load_scale_rows(w_plane, w4_scales, 4)
-        l_pos3 = load_list(pos3, "l_pos3")
-        t1.append(load_words(tab_words[1], "t1b"))
-        load_scale_rows(tab_plane, tab_scales, 0)
+        load_scale_rows(w2_plane, w2_scales, 0)
+        t3 = load_words(tab3_words[0], "t3")
+        l_offs3 = load_list(offs3, "l_offs3")
+        load_scale_rows(tab3_plane, tab3_scales, 0)
+        w3_raw = [load_weight(w3, 0, 0)]
         l_pos2 = load_list(pos2, "l_pos2")
-        l_pos1 = load_list(pos1, "l_pos1")
+        w3_raw.append(load_weight(w3, 0, 1))
+        l_offs = load_list(offs, "l_offs")
+        t1 = [load_words(tab_words[0], "t1a"), load_words(tab_words[1], "t1b")]
+        load_scale_rows(tab_plane, tab_scales, 0)
+        l_pos3 = load_list(pos3, "l_pos3")
         w1_raw = {}
         for b in range(HALVES):
             for a in range(K // K_PASS):
                 w1_raw[a, b] = load_weight(w1, a, b)
+        l_pos1 = load_list(pos1, "l_pos1")
+        load_scale_rows(w4_plane, w4_scales, 0)
         gain = keep.tile([P, HALVES, PACK], F32, name="gain")
         nc.sync.dma_start(gain[:], gd.rearrange("(b p t) -> p b t", p=P, t=PACK))
         w4_raw = keep.tile([P, 2, H], I32, name="w4_raw", align_bytes=64)
         nc.sync.dma_start(w4_raw[:], w4_words.rearrange("a p c i -> p a (c i)").bitcast(I32))
 
-        v3 = gather_words(t3, l_offs3, "v3")
-        v3_plane = gather_scales(tab3_plane, l_offs3, "v3_plane")
-        w3_q = [quantize(cast_weight(w3_raw[0]), "w3_0")]
-        v2 = gather_words(t2, l_offs2, "v2")
-        v2_plane = gather_scales(tab2_plane, l_offs2, "v2_plane")
-        w3_q.append(quantize(cast_weight(w3_raw[1]), "w3_1"))
-
-        w2_dealt = keep.tile([P, 2 * H], U8, name="w2_dealt", align_bytes=64)
-        w_plane_dealt = keep.tile([P, H], U8, name="w_plane_dealt", align_bytes=64)
-        for b in range(HALVES):
+        def deal_plane(plane, dealt, b):
             cols = slice(K_PASS * b, K_PASS * (b + 1))
+            nc.gpsimd.tensor_copy(
+                dealt[:, cols].rearrange("p (t q) -> p t q", t=PACK),
+                plane[:, cols].rearrange("p (q t) -> p t q", t=PACK),
+            )
+
+        v2_plane = gather_scales(tab2_plane, l_offs2, "v2_plane")
+        v2 = gather_words(t2, l_offs2, "v2")
+        w2_dealt = keep.tile([P, 2 * H], U8, name="w2_dealt", align_bytes=64)
+        w2_plane_dealt = keep.tile([P, H], U8, name="w2_plane_dealt", align_bytes=64)
+        for b in range(HALVES):
             two = slice(2 * K_PASS * b, 2 * K_PASS * (b + 1))
             nc.gpsimd.tensor_copy(
                 w2_dealt[:, two].rearrange("p (t q e) -> p t q e", t=PACK, e=2),
                 w2_raw[:, two].rearrange("p (q t e) -> p t q e", t=PACK, e=2),
             )
-            nc.gpsimd.tensor_copy(
-                w_plane_dealt[:, cols].rearrange("p (t q) -> p t q", t=PACK),
-                w_plane[:, cols].rearrange("p (q t) -> p t q", t=PACK),
-            )
-
+            deal_plane(w2_plane, w2_plane_dealt, b)
+        v3 = gather_words(t3, l_offs3, "v3")
+        v3_plane = gather_scales(tab3_plane, l_offs3, "v3_plane")
+        w3_q = [quantize(cast_weight(w3_raw[b], True), "w3_%d" % b) for b in range(HALVES)]
         v1 = [gather_words(t1[0], l_offs, "v1a"), gather_words(t1[1], l_offs, "v1b")]
         v1_plane = gather_scales(tab_plane, l_offs, "v1_plane")
+        w1_q = {}
+        for b in range(HALVES):
+            for a in range(K // K_PASS):
+                w1_q[a, b] = quantize(cast_weight(w1_raw[a, b], False), "w1_%d%d" % (a, b))
 
         d_picked = [keep.tile([P, PACK, J], F32, name="d_picked%d" % b, align_bytes=64) for b in range(HALVES)]
         best = [keep.tile([P, PACK, J], F32, name="best%d" % b, align_bytes=64) for b in range(HALVES)]
@@ -167,78 +174,82 @@ def tile_list_carton_seal_join_kernel(
 
         def slice_b(b, t):
             lo = K_PASS * b + P * t
-            window = first_stage([(w2_dealt[:, 2 * lo : 2 * (lo + P)].bitcast(FP4X4), w_plane_dealt[:, lo : lo + P], v2, v2_plane, 0)])
+            window = first_stage([(w2_dealt[:, 2 * lo : 2 * (lo + P)].bitcast(FP4X4), w2_plane_dealt[:, lo : lo + P], v2, v2_plane, 0)])
             nc.vector.tensor_copy(best[b][:, t, :], window[:].indirect(l_pos2[:]))
 
-        w1_q = {}
-
-        def slice_a(b, t):
+        def window_a(b, t):
             cols = slice(P * t, P * (t + 1))
-            window = first_stage([
+            return first_stage([
                 (w1_q[a, b][0][:, cols].bitcast(FP8X4), w1_q[a, b][1][:, cols], v1[a], v1_plane, 4 * a)
                 for a in range(K // K_PASS)
             ])
-            a_picked = ring.tile([P, J], F32, name="a_picked", tag="a_picked", bufs=2, align_bytes=64)
-            nc.vector.tensor_copy(a_picked[:], window[:].indirect(l_pos1[:]))
-            nc.vector.tensor_tensor(best[b][:, t, :], a_picked[:], best[b][:, t, :], ALU.max)
 
-        def join(b):
+        def absolute(b):
             d_abs = ring.tile([P, PACK, J], F32, name="d_abs", tag="raw", bufs=4, align_bytes=64)
             nc.scalar.activation(d_abs[:], d_picked[b][:], ACT.Abs)
-            grouped = ring.tile([P, PACK * J], BF16, name="grouped", tag="grouped", bufs=3, align_bytes=64)
+            return d_abs
+
+        def join(b, windows, d_abs, lo, width):
+            cols = slice(lo, lo + width)
+            a_picked = ring.tile([P, PACK, width], F32, name="a_picked", tag="a_picked", bufs=1, align_bytes=64)
+            for t in range(PACK):
+                nc.vector.tensor_copy(a_picked[:, t, :], windows[t][:].indirect(l_pos1[:, lo // 16 : (lo + width) // 16]))
+            nc.vector.tensor_tensor(best[b][:, :, cols], a_picked[:], best[b][:, :, cols], ALU.max)
+            grouped = ring.tile([P, PACK * width], BF16, name="grouped", tag="grouped", bufs=5, align_bytes=64)
             nc.vector.tensor_tensor(
                 grouped[:].rearrange("p (c i t) -> p c t i", i=4, t=PACK),
-                best[b][:].rearrange("p t (c i) -> p c t i", i=4),
-                d_abs[:].rearrange("p t (c i) -> p c t i", i=4),
+                best[b][:, :, cols].rearrange("p t (c i) -> p c t i", i=4),
+                d_abs[:, :, cols].rearrange("p t (c i) -> p c t i", i=4),
                 ALU.subtract,
             )
-            return quantize(grouped, "z%d" % b)
+            return quantize(grouped, "z%d_%d" % (b, lo))
 
-        for t in range(PACK):
-            slice_d(0, t)
-        for t in range(PACK):
-            slice_b(0, t)
-        for a in range(K // K_PASS):
-            w1_q[a, 0] = quantize(cast_weight(w1_raw[a, 0]), "w1_%d0" % a)
-        for t in range(PACK):
-            slice_d(1, t)
-        for a in range(K // K_PASS):
-            w1_q[a, 1] = quantize(cast_weight(w1_raw[a, 1]), "w1_%d1" % a)
-        for t in range(PACK):
-            slice_b(1, t)
-        for t in range(PACK):
-            slice_a(0, t)
-        z_q = [join(0)]
+        for b in range(HALVES):
+            for t in range(PACK):
+                slice_b(b, t)
+        for b in range(HALVES):
+            for t in range(PACK):
+                slice_d(b, t)
+        windows = [window_a(0, t) for t in range(PACK)]
+        z0 = join(0, windows, absolute(0), 0, J)
 
         w4_dealt = keep.tile([P, 2, H], I32, name="w4_dealt", align_bytes=64)
-        for a in range(HALVES):
-            for b in range(HALVES):
+        w4_plane_dealt = keep.tile([P, H], U8, name="w4_plane_dealt", align_bytes=64)
+        for b in range(HALVES):
+            deal_plane(w4_plane, w4_plane_dealt, b)
+            for a in range(HALVES):
                 cols = slice(K_PASS * b, K_PASS * (b + 1))
                 nc.gpsimd.tensor_copy(
                     w4_dealt[:, a, cols].rearrange("p (t q) -> p t q", t=PACK),
                     w4_raw[:, a, cols].rearrange("p (q t) -> p t q", t=PACK),
                 )
 
-        for t in range(PACK):
-            slice_a(1, t)
-        z_q.append(join(1))
+        windows = [window_a(1, t) for t in range(PACK)]
+        d_abs = absolute(1)
+        part = J // 2
+        z1 = [join(1, windows, d_abs, lo, part) for lo in range(0, J, part)]
 
         out_rows = out.rearrange("(b p t) j -> b p t j", p=P, t=PACK)
-        for b in range(HALVES):
-            result = ring.tile([P, PACK, J], F32, name="result", tag="raw", bufs=4, align_bytes=64)
-            for t in range(PACK):
-                lo = K_PASS * b + P * t
-                acc = psum.tile([P, J], F32, name="acc", tag="acc")
-                for a in range(HALVES):
-                    nc.tensor.matmul_mx(
-                        out=acc[:], lhsT=w4_dealt[:, a, lo : lo + P].bitcast(FP8X4),
-                        lhsT_scale=w_plane_dealt[4 + 4 * a : P, lo : lo + P],
-                        rhs=z_q[a][0][:].bitcast(FP8X4), rhs_scale=z_q[a][1][:],
-                        start=(a == 0), stop=(a == HALVES - 1),
-                    )
-                summed = ring.tile([P, J], F32, name="summed", tag="a_picked", bufs=2, align_bytes=64)
-                nc.vector.scalar_tensor_tensor(
-                    summed[:], d_picked[b][:, t, :], gain[:, b, t : t + 1], acc[:], ALU.mult, ALU.add
-                )
-                nc.scalar.activation(result[:, t, :], summed[:], ACT.Tanh)
-                nc.sync.dma_start(out_rows[b, :, t, :], result[:, t, :])
+        for h in range(J // part):
+            cols = slice(h * part, (h + 1) * part)
+            moving = [(z0[0][:, cols], z0[1][:, cols]), (z1[h][0][:], z1[h][1][:])]
+            for b in range(HALVES):
+                for pair in range(0, PACK, 2):
+                    summed = ring.tile([P, 2, part], F32, name="summed", tag="summed", bufs=3, align_bytes=64)
+                    for u in range(2):
+                        t = pair + u
+                        lo = K_PASS * b + P * t
+                        acc = psum.tile([P, part], F32, name="acc", tag="acc")
+                        for a in range(HALVES):
+                            nc.tensor.matmul_mx(
+                                out=acc[:], lhsT=w4_dealt[:, a, lo : lo + P].bitcast(FP8X4),
+                                lhsT_scale=w4_plane_dealt[4 * a : P, lo : lo + P],
+                                rhs=moving[a][0].bitcast(FP8X4), rhs_scale=moving[a][1],
+                                start=(a == 0), stop=(a == HALVES - 1),
+                            )
+                        nc.vector.scalar_tensor_tensor(
+                            summed[:, u, :], d_picked[b][:, t, cols], gain[:, b, t : t + 1], acc[:], ALU.mult, ALU.add
+                        )
+                    result = ring.tile([P, 2, part], F32, name="result", tag="window", bufs=8, align_bytes=64)
+                    nc.scalar.activation(result[:], summed[:], ACT.Tanh)
+                    nc.sync.dma_start(out_rows[b, :, pair : pair + 2, cols], result[:])

@@ -40,7 +40,7 @@ def tile_list_carton_seal_join_kernel(
             return tile
 
         def load_words(src, name):
-            tile = keep.tile([P, T], I32, name=name, align_bytes=64)
+            tile = ring.tile([P, T], I32, name=name, tag=name, bufs=1, align_bytes=64)
             nc.sync.dma_start(tile[:], src.rearrange("p t i -> p (t i)").bitcast(I32))
             return tile
 
@@ -49,16 +49,18 @@ def tile_list_carton_seal_join_kernel(
             engine.memset(tile[:].bitcast(I32), 0)
             return tile
 
-        def load_scale_rows(plane, src, first_row):
+        def load_scale_rows(plane, src, first_row, queue=nc.sync):
             rows = 4 * src.shape[0]
             for quad in range(QUADS):
                 lo = 32 * quad + first_row
-                nc.sync.dma_start(plane[lo : lo + rows, :].bitcast(I32), src[:, 4 * quad : 4 * quad + 4, :].bitcast(I32))
+                queue.dma_start(plane[lo : lo + rows, :].bitcast(I32), src[:, 4 * quad : 4 * quad + 4, :].bitcast(I32))
 
-        def load_weight(src, a, b):
-            raw = ring.tile([P, PACK, K_PASS], F32, name="raw", tag="raw", bufs=4, align_bytes=64)
-            rows = src[K_PASS * a : K_PASS * (a + 1), K_PASS * b : K_PASS * (b + 1)]
-            nc.sync.dma_start(raw[:], rows.rearrange("(p j) c -> p j c", j=PACK))
+        def load_weight(src, a, b, pieces=1):
+            raw = ring.tile([P, PACK, K_PASS], F32, name="raw", tag="raw", bufs=6, align_bytes=64)
+            rows = src[K_PASS * a : K_PASS * (a + 1), K_PASS * b : K_PASS * (b + 1)].rearrange("(p j) c -> p j c", j=PACK)
+            step = K_PASS // pieces
+            for lo in range(0, K_PASS, step):
+                nc.sync.dma_start(raw[:, :, lo : lo + step], rows[:, :, lo : lo + step])
             return raw
 
         def gather_words(table, offsets, name):
@@ -71,15 +73,15 @@ def tile_list_carton_seal_join_kernel(
             nc.vector.tensor_copy(picked[:], plane[:].indirect(offsets[:]))
             return picked
 
-        def cast_weight(raw, on_scalar):
-            grouped = ring.tile([P, PACK * K_PASS], BF16, name="grouped", tag="grouped", bufs=5, align_bytes=64)
-            dst = grouped[:].rearrange("p (t q j) -> p q t j", t=PACK, j=PACK)
+        def cast_weight(raw, grouped, on_scalar, pieces=1):
+            dst = grouped.rearrange("p (t q j) -> p q t j", t=PACK, j=PACK)
             src = raw[:].rearrange("p j (q t) -> p q t j", t=PACK)
-            if on_scalar:
-                nc.scalar.copy(dst, src)
-            else:
-                nc.gpsimd.tensor_scalar(dst, src, 1.0, 0.0, ALU.mult, ALU.add)
-            return grouped
+            step = P // pieces
+            for lo in range(0, P, step):
+                if on_scalar:
+                    nc.scalar.copy(dst[:, lo : lo + step], src[:, lo : lo + step])
+                else:
+                    nc.gpsimd.tensor_scalar(dst[:, lo : lo + step], src[:, lo : lo + step], 1.0, 0.0, ALU.mult, ALU.add)
 
         def quantize(grouped, name):
             width = grouped.shape[1] // PACK
@@ -89,7 +91,7 @@ def tile_list_carton_seal_join_kernel(
             return codes, scales
 
         def first_stage(passes):
-            window = ring.tile([P, S], F32, name="window", tag="window", bufs=8, align_bytes=64)
+            window = ring.tile([P, S], F32, name="window", tag="window", bufs=12, align_bytes=64)
             for h in range(S // N_BANK):
                 cols = slice(h * N_BANK, (h + 1) * N_BANK)
                 acc = psum.tile([P, N_BANK], F32, name="acc", tag="acc")
@@ -102,38 +104,38 @@ def tile_list_carton_seal_join_kernel(
                 nc.scalar.copy(window[:, cols], acc[:])
             return window
 
-        tab2_plane = zeroed_plane(T, "tab2_plane", nc.gpsimd)
+        tab3_plane = zeroed_plane(T, "tab3_plane", nc.gpsimd)
+        tab2_plane = zeroed_plane(T, "tab2_plane", nc.vector)
         w2_plane = zeroed_plane(H, "w2_plane", nc.vector)
-        tab3_plane = zeroed_plane(T, "tab3_plane", nc.vector)
         tab_plane = zeroed_plane(T, "tab_plane", nc.vector)
         w4_plane = zeroed_plane(H, "w4_plane", nc.gpsimd)
 
+        l_offs3 = load_list(offs3, "l_offs3")
+        t3 = load_words(tab3_words[0], "t3")
+        load_scale_rows(tab3_plane, tab3_scales, 0, nc.scalar)
+        w3_raw = [load_weight(w3, 0, 0, 2)]
         l_offs2 = load_list(offs2, "l_offs2")
-        load_scale_rows(tab2_plane, tab2_scales, 0)
         t2 = load_words(tab2_words[0], "t2")
+        load_scale_rows(tab2_plane, tab2_scales, 0)
+        w3_raw.append(load_weight(w3, 0, 1))
         w2_raw = keep.tile([P, 2 * H], U8, name="w2_raw", align_bytes=64)
         nc.sync.dma_start(w2_raw[:].bitcast(I32), w2_words[0].bitcast(I32))
         load_scale_rows(w2_plane, w2_scales, 0)
-        t3 = load_words(tab3_words[0], "t3")
-        l_offs3 = load_list(offs3, "l_offs3")
-        load_scale_rows(tab3_plane, tab3_scales, 0)
-        w3_raw = [load_weight(w3, 0, 0)]
-        l_pos2 = load_list(pos2, "l_pos2")
-        w3_raw.append(load_weight(w3, 0, 1))
-        l_offs = load_list(offs, "l_offs")
-        t1 = [load_words(tab_words[0], "t1a"), load_words(tab_words[1], "t1b")]
-        load_scale_rows(tab_plane, tab_scales, 0)
+        t1 = [load_words(tab_words[0], "t1a")]
         l_pos3 = load_list(pos3, "l_pos3")
-        w1_raw = {}
-        for b in range(HALVES):
-            for a in range(K // K_PASS):
-                w1_raw[a, b] = load_weight(w1, a, b)
-        l_pos1 = load_list(pos1, "l_pos1")
+        l_offs = load_list(offs, "l_offs")
+        w1_raw = {(a, 0): load_weight(w1, a, 0) for a in range(K // K_PASS)}
+        load_scale_rows(tab_plane, tab_scales, 0)
+        t1.append(load_words(tab_words[1], "t1b"))
+        for a in range(K // K_PASS):
+            w1_raw[a, 1] = load_weight(w1, a, 1)
         load_scale_rows(w4_plane, w4_scales, 0)
-        gain = keep.tile([P, HALVES, PACK], F32, name="gain")
-        nc.sync.dma_start(gain[:], gd.rearrange("(b p t) -> p b t", p=P, t=PACK))
         w4_raw = keep.tile([P, 2, H], I32, name="w4_raw", align_bytes=64)
         nc.sync.dma_start(w4_raw[:], w4_words.rearrange("a p c i -> p a (c i)").bitcast(I32))
+        l_pos2 = load_list(pos2, "l_pos2")
+        l_pos1 = load_list(pos1, "l_pos1")
+        gain = keep.tile([P, HALVES, PACK], F32, name="gain")
+        nc.sync.dma_start(gain[:], gd.rearrange("(b p t) -> p b t", p=P, t=PACK))
 
         def deal_plane(plane, dealt, b):
             cols = slice(K_PASS * b, K_PASS * (b + 1))
@@ -142,8 +144,15 @@ def tile_list_carton_seal_join_kernel(
                 plane[:, cols].rearrange("p (q t) -> p t q", t=PACK),
             )
 
-        v2_plane = gather_scales(tab2_plane, l_offs2, "v2_plane")
+        v3_plane = gather_scales(tab3_plane, l_offs3, "v3_plane")
+        v3 = gather_words(t3, l_offs3, "v3")
+        w3_q = []
+        for b in range(HALVES):
+            grouped = ring.tile([P, PACK * K_PASS], BF16, name="grouped", tag="grouped", bufs=2, align_bytes=64)
+            cast_weight(w3_raw[b], grouped[:], True, 2 - b)
+            w3_q.append(quantize(grouped, "w3_%d" % b))
         v2 = gather_words(t2, l_offs2, "v2")
+        v2_plane = gather_scales(tab2_plane, l_offs2, "v2_plane")
         w2_dealt = keep.tile([P, 2 * H], U8, name="w2_dealt", align_bytes=64)
         w2_plane_dealt = keep.tile([P, H], U8, name="w2_plane_dealt", align_bytes=64)
         for b in range(HALVES):
@@ -153,18 +162,23 @@ def tile_list_carton_seal_join_kernel(
                 w2_raw[:, two].rearrange("p (q t e) -> p t q e", t=PACK, e=2),
             )
             deal_plane(w2_plane, w2_plane_dealt, b)
-        v3 = gather_words(t3, l_offs3, "v3")
-        v3_plane = gather_scales(tab3_plane, l_offs3, "v3_plane")
-        w3_q = [quantize(cast_weight(w3_raw[b], True), "w3_%d" % b) for b in range(HALVES)]
         v1 = [gather_words(t1[0], l_offs, "v1a"), gather_words(t1[1], l_offs, "v1b")]
         v1_plane = gather_scales(tab_plane, l_offs, "v1_plane")
+
         w1_q = {}
-        for b in range(HALVES):
-            for a in range(K // K_PASS):
-                w1_q[a, b] = quantize(cast_weight(w1_raw[a, b], False), "w1_%d%d" % (a, b))
+
+        def quantize_w1():
+            width = PACK * K_PASS
+            wide = [ring.tile([P, 2 * width], BF16, name="w1_wide", tag=tag, bufs=1, align_bytes=64) for tag in ("t3", "t2")]
+            place = {(0, 0): (0, 0), (1, 0): (1, 0), (0, 1): (1, 1), (1, 1): (0, 1)}
+            for key, (i, u) in place.items():
+                cast_weight(w1_raw[key], wide[i][:, u * width : (u + 1) * width], False, 2)
+            done = [quantize(wide[i], "w1_%d" % i) for i in range(2)]
+            for key, (i, u) in place.items():
+                cols = slice(u * K_PASS, (u + 1) * K_PASS)
+                w1_q[key] = (done[i][0][:, cols], done[i][1][:, cols])
 
         d_picked = [keep.tile([P, PACK, J], F32, name="d_picked%d" % b, align_bytes=64) for b in range(HALVES)]
-        best = [keep.tile([P, PACK, J], F32, name="best%d" % b, align_bytes=64) for b in range(HALVES)]
 
         def slice_d(b, t):
             cols = slice(P * t, P * (t + 1))
@@ -175,7 +189,7 @@ def tile_list_carton_seal_join_kernel(
         def slice_b(b, t):
             lo = K_PASS * b + P * t
             window = first_stage([(w2_dealt[:, 2 * lo : 2 * (lo + P)].bitcast(FP4X4), w2_plane_dealt[:, lo : lo + P], v2, v2_plane, 0)])
-            nc.vector.tensor_copy(best[b][:, t, :], window[:].indirect(l_pos2[:]))
+            nc.vector.tensor_tensor(best[b][:, t, :], window[:].indirect(l_pos2[:]), d_abs[b][:, t, :], ALU.subtract)
 
         def window_a(b, t):
             cols = slice(P * t, P * (t + 1))
@@ -185,34 +199,29 @@ def tile_list_carton_seal_join_kernel(
             ])
 
         def absolute(b):
-            d_abs = ring.tile([P, PACK, J], F32, name="d_abs", tag="raw", bufs=4, align_bytes=64)
+            d_abs = ring.tile([P, PACK, J], F32, name="d_abs", tag="raw", bufs=6, align_bytes=64)
             nc.scalar.activation(d_abs[:], d_picked[b][:], ACT.Abs)
             return d_abs
 
         def join(b, windows, d_abs, lo, width):
             cols = slice(lo, lo + width)
-            a_picked = ring.tile([P, PACK, width], F32, name="a_picked", tag="a_picked", bufs=1, align_bytes=64)
+            a_picked = ring.tile([P, PACK, width], F32, name="a_picked", tag="t1a", bufs=1, align_bytes=64)
             for t in range(PACK):
-                nc.vector.tensor_copy(a_picked[:, t, :], windows[t][:].indirect(l_pos1[:, lo // 16 : (lo + width) // 16]))
-            nc.vector.tensor_tensor(best[b][:, :, cols], a_picked[:], best[b][:, :, cols], ALU.max)
-            grouped = ring.tile([P, PACK * width], BF16, name="grouped", tag="grouped", bufs=5, align_bytes=64)
+                picked = windows[t][:].indirect(l_pos1[:, lo // 16 : (lo + width) // 16])
+                nc.vector.tensor_tensor(a_picked[:, t, :], picked, d_abs[:, t, cols], ALU.subtract)
+            grouped = ring.tile([P, PACK * width], BF16, name="grouped", tag="grouped", bufs=2, align_bytes=64)
             nc.vector.tensor_tensor(
                 grouped[:].rearrange("p (c i t) -> p c t i", i=4, t=PACK),
+                a_picked[:].rearrange("p t (c i) -> p c t i", i=4),
                 best[b][:, :, cols].rearrange("p t (c i) -> p c t i", i=4),
-                d_abs[:, :, cols].rearrange("p t (c i) -> p c t i", i=4),
-                ALU.subtract,
+                ALU.max,
             )
             return quantize(grouped, "z%d_%d" % (b, lo))
 
         for b in range(HALVES):
             for t in range(PACK):
-                slice_b(b, t)
-        for b in range(HALVES):
-            for t in range(PACK):
                 slice_d(b, t)
-        windows = [window_a(0, t) for t in range(PACK)]
-        z0 = join(0, windows, absolute(0), 0, J)
-
+        quantize_w1()
         w4_dealt = keep.tile([P, 2, H], I32, name="w4_dealt", align_bytes=64)
         w4_plane_dealt = keep.tile([P, H], U8, name="w4_plane_dealt", align_bytes=64)
         for b in range(HALVES):
@@ -224,32 +233,45 @@ def tile_list_carton_seal_join_kernel(
                     w4_raw[:, a, cols].rearrange("p (q t) -> p t q", t=PACK),
                 )
 
+        best = [
+            keep.tile([P, PACK, J], F32, name="best0", align_bytes=64),
+            ring.tile([P, PACK, J], F32, name="best1", tag="t3", bufs=1, align_bytes=64),
+        ]
+        d_abs = []
+        for b in range(HALVES):
+            d_abs.append(absolute(b))
+            for t in range(PACK):
+                slice_b(b, t)
+        z0 = join(0, [window_a(0, t) for t in range(PACK)], d_abs[0], 0, J)
         windows = [window_a(1, t) for t in range(PACK)]
-        d_abs = absolute(1)
         part = J // 2
-        z1 = [join(1, windows, d_abs, lo, part) for lo in range(0, J, part)]
+        z1 = [join(1, windows, d_abs[1], lo, part) for lo in range(0, J, part)]
 
         out_rows = out.rearrange("(b p t) j -> b p t j", p=P, t=PACK)
         for h in range(J // part):
             cols = slice(h * part, (h + 1) * part)
             moving = [(z0[0][:, cols], z0[1][:, cols]), (z1[h][0][:], z1[h][1][:])]
+            accs = [psum.tile([P, part], F32, name="acc", tag="acc") for n in range(H // P)]
+
+            def y_pass(n, a):
+                nc.tensor.matmul_mx(
+                    out=accs[n][:], lhsT=w4_dealt[:, a, P * n : P * (n + 1)].bitcast(FP8X4),
+                    lhsT_scale=w4_plane_dealt[4 * a : P, P * n : P * (n + 1)],
+                    rhs=moving[a][0].bitcast(FP8X4), rhs_scale=moving[a][1],
+                    start=(a == 0), stop=(a == HALVES - 1),
+                )
+
+            for n in range(H // P):
+                y_pass(n, 0)
             for b in range(HALVES):
                 for pair in range(0, PACK, 2):
                     summed = ring.tile([P, 2, part], F32, name="summed", tag="summed", bufs=3, align_bytes=64)
                     for u in range(2):
                         t = pair + u
-                        lo = K_PASS * b + P * t
-                        acc = psum.tile([P, part], F32, name="acc", tag="acc")
-                        for a in range(HALVES):
-                            nc.tensor.matmul_mx(
-                                out=acc[:], lhsT=w4_dealt[:, a, lo : lo + P].bitcast(FP8X4),
-                                lhsT_scale=w4_plane_dealt[4 * a : P, lo : lo + P],
-                                rhs=moving[a][0].bitcast(FP8X4), rhs_scale=moving[a][1],
-                                start=(a == 0), stop=(a == HALVES - 1),
-                            )
+                        y_pass(PACK * b + t, 1)
                         nc.vector.scalar_tensor_tensor(
-                            summed[:, u, :], d_picked[b][:, t, cols], gain[:, b, t : t + 1], acc[:], ALU.mult, ALU.add
+                            summed[:, u, :], d_picked[b][:, t, cols], gain[:, b, t : t + 1], accs[PACK * b + t][:], ALU.mult, ALU.add
                         )
-                    result = ring.tile([P, 2, part], F32, name="result", tag="window", bufs=8, align_bytes=64)
+                    result = ring.tile([P, 2, part], F32, name="result", tag="window", bufs=12, align_bytes=64)
                     nc.scalar.activation(result[:], summed[:], ACT.Tanh)
                     nc.sync.dma_start(out_rows[b, :, pair : pair + 2, cols], result[:])

@@ -106,32 +106,31 @@ def tile_list_carton_seal_join_kernel(
 
         tab3_plane = zeroed_plane(T, "tab3_plane", nc.gpsimd)
         tab2_plane = zeroed_plane(T, "tab2_plane", nc.vector)
-        w2_plane = zeroed_plane(H, "w2_plane", nc.vector)
+        w_plane = zeroed_plane(H, "w_plane", nc.vector)
         tab_plane = zeroed_plane(T, "tab_plane", nc.vector)
-        w4_plane = zeroed_plane(H, "w4_plane", nc.gpsimd)
 
         l_offs3 = load_list(offs3, "l_offs3")
         t3 = load_words(tab3_words[0], "t3")
-        load_scale_rows(tab3_plane, tab3_scales, 0, nc.scalar)
+        load_scale_rows(tab3_plane, tab3_scales, 12, nc.scalar)
         w3_raw = [load_weight(w3, 0, 0, 2)]
         l_offs2 = load_list(offs2, "l_offs2")
         t2 = load_words(tab2_words[0], "t2")
         load_scale_rows(tab2_plane, tab2_scales, 0)
         w3_raw.append(load_weight(w3, 0, 1))
+        l_pos3 = load_list(pos3, "l_pos3")
         w2_raw = keep.tile([P, 2 * H], U8, name="w2_raw", align_bytes=64)
         nc.sync.dma_start(w2_raw[:].bitcast(I32), w2_words[0].bitcast(I32))
-        load_scale_rows(w2_plane, w2_scales, 0)
-        t1 = [load_words(tab_words[0], "t1a")]
-        l_pos3 = load_list(pos3, "l_pos3")
-        l_offs = load_list(offs, "l_offs")
-        w1_raw = {(a, 0): load_weight(w1, a, 0) for a in range(K // K_PASS)}
-        load_scale_rows(tab_plane, tab_scales, 0)
-        t1.append(load_words(tab_words[1], "t1b"))
-        for a in range(K // K_PASS):
-            w1_raw[a, 1] = load_weight(w1, a, 1)
-        load_scale_rows(w4_plane, w4_scales, 0)
+        load_scale_rows(w_plane, w2_scales, 0)
         w4_raw = keep.tile([P, 2, H], I32, name="w4_raw", align_bytes=64)
         nc.sync.dma_start(w4_raw[:], w4_words.rearrange("a p c i -> p a (c i)").bitcast(I32))
+        load_scale_rows(w_plane, w4_scales, 8)
+        l_offs = load_list(offs, "l_offs")
+        t1 = [load_words(tab_words[0], "t1a")]
+        w1_raw = {(a, 0): load_weight(w1, a, 0) for a in range(K // K_PASS)}
+        load_scale_rows(tab_plane, tab_scales, 4)
+        for a in range(K // K_PASS):
+            w1_raw[a, 1] = load_weight(w1, a, 1)
+        t1.append(load_words(tab_words[1], "t1b"))
         l_pos2 = load_list(pos2, "l_pos2")
         l_pos1 = load_list(pos1, "l_pos1")
         gain = keep.tile([P, HALVES, PACK], F32, name="gain")
@@ -154,16 +153,25 @@ def tile_list_carton_seal_join_kernel(
         v2 = gather_words(t2, l_offs2, "v2")
         v2_plane = gather_scales(tab2_plane, l_offs2, "v2_plane")
         w2_dealt = keep.tile([P, 2 * H], U8, name="w2_dealt", align_bytes=64)
-        w2_plane_dealt = keep.tile([P, H], U8, name="w2_plane_dealt", align_bytes=64)
         for b in range(HALVES):
             two = slice(2 * K_PASS * b, 2 * K_PASS * (b + 1))
             nc.gpsimd.tensor_copy(
                 w2_dealt[:, two].rearrange("p (t q e) -> p t q e", t=PACK, e=2),
                 w2_raw[:, two].rearrange("p (q t e) -> p t q e", t=PACK, e=2),
             )
-            deal_plane(w2_plane, w2_plane_dealt, b)
         v1 = [gather_words(t1[0], l_offs, "v1a"), gather_words(t1[1], l_offs, "v1b")]
         v1_plane = gather_scales(tab_plane, l_offs, "v1_plane")
+
+        w4_dealt = keep.tile([P, 2, H], I32, name="w4_dealt", align_bytes=64)
+        w_plane_dealt = keep.tile([P, H], U8, name="w_plane_dealt", align_bytes=64)
+        for b in range(HALVES):
+            deal_plane(w_plane, w_plane_dealt, b)
+            for a in range(HALVES):
+                cols = slice(K_PASS * b, K_PASS * (b + 1))
+                nc.gpsimd.tensor_copy(
+                    w4_dealt[:, a, cols].rearrange("p (t q) -> p t q", t=PACK),
+                    w4_raw[:, a, cols].rearrange("p (q t) -> p t q", t=PACK),
+                )
 
         w1_q = {}
 
@@ -183,18 +191,18 @@ def tile_list_carton_seal_join_kernel(
         def slice_d(b, t):
             cols = slice(P * t, P * (t + 1))
             codes, scales = w3_q[b]
-            window = first_stage([(codes[:, cols].bitcast(FP8X4), scales[:, cols], v3, v3_plane, 0)])
+            window = first_stage([(codes[:, cols].bitcast(FP8X4), scales[:, cols], v3, v3_plane, 12)])
             nc.vector.tensor_copy(d_picked[b][:, t, :], window[:].indirect(l_pos3[:]))
 
         def slice_b(b, t):
             lo = K_PASS * b + P * t
-            window = first_stage([(w2_dealt[:, 2 * lo : 2 * (lo + P)].bitcast(FP4X4), w2_plane_dealt[:, lo : lo + P], v2, v2_plane, 0)])
+            window = first_stage([(w2_dealt[:, 2 * lo : 2 * (lo + P)].bitcast(FP4X4), w_plane_dealt[:, lo : lo + P], v2, v2_plane, 0)])
             nc.vector.tensor_tensor(best[b][:, t, :], window[:].indirect(l_pos2[:]), d_abs[b][:, t, :], ALU.subtract)
 
         def window_a(b, t):
             cols = slice(P * t, P * (t + 1))
             return first_stage([
-                (w1_q[a, b][0][:, cols].bitcast(FP8X4), w1_q[a, b][1][:, cols], v1[a], v1_plane, 4 * a)
+                (w1_q[a, b][0][:, cols].bitcast(FP8X4), w1_q[a, b][1][:, cols], v1[a], v1_plane, 4 + 4 * a)
                 for a in range(K // K_PASS)
             ])
 
@@ -222,17 +230,6 @@ def tile_list_carton_seal_join_kernel(
             for t in range(PACK):
                 slice_d(b, t)
         quantize_w1()
-        w4_dealt = keep.tile([P, 2, H], I32, name="w4_dealt", align_bytes=64)
-        w4_plane_dealt = keep.tile([P, H], U8, name="w4_plane_dealt", align_bytes=64)
-        for b in range(HALVES):
-            deal_plane(w4_plane, w4_plane_dealt, b)
-            for a in range(HALVES):
-                cols = slice(K_PASS * b, K_PASS * (b + 1))
-                nc.gpsimd.tensor_copy(
-                    w4_dealt[:, a, cols].rearrange("p (t q) -> p t q", t=PACK),
-                    w4_raw[:, a, cols].rearrange("p (q t) -> p t q", t=PACK),
-                )
-
         best = [
             keep.tile([P, PACK, J], F32, name="best0", align_bytes=64),
             ring.tile([P, PACK, J], F32, name="best1", tag="t3", bufs=1, align_bytes=64),
@@ -251,27 +248,31 @@ def tile_list_carton_seal_join_kernel(
         for h in range(J // part):
             cols = slice(h * part, (h + 1) * part)
             moving = [(z0[0][:, cols], z0[1][:, cols]), (z1[h][0][:], z1[h][1][:])]
+            group = 2 if h == 0 else 1
             accs = [psum.tile([P, part], F32, name="acc", tag="acc") for n in range(H // P)]
 
             def y_pass(n, a):
                 nc.tensor.matmul_mx(
                     out=accs[n][:], lhsT=w4_dealt[:, a, P * n : P * (n + 1)].bitcast(FP8X4),
-                    lhsT_scale=w4_plane_dealt[4 * a : P, P * n : P * (n + 1)],
+                    lhsT_scale=w_plane_dealt[8 + 4 * a : P, P * n : P * (n + 1)],
                     rhs=moving[a][0].bitcast(FP8X4), rhs_scale=moving[a][1],
                     start=(a == 0), stop=(a == HALVES - 1),
                 )
 
-            for n in range(H // P):
-                y_pass(n, 0)
+            if h == 0:
+                for n in range(H // P):
+                    y_pass(n, 0)
             for b in range(HALVES):
-                for pair in range(0, PACK, 2):
-                    summed = ring.tile([P, 2, part], F32, name="summed", tag="summed", bufs=3, align_bytes=64)
-                    for u in range(2):
+                for pair in range(0, PACK, group):
+                    summed = ring.tile([P, group, part], F32, name="summed", tag="summed", bufs=4, align_bytes=64)
+                    for u in range(group):
                         t = pair + u
+                        if h > 0:
+                            y_pass(PACK * b + t, 0)
                         y_pass(PACK * b + t, 1)
                         nc.vector.scalar_tensor_tensor(
                             summed[:, u, :], d_picked[b][:, t, cols], gain[:, b, t : t + 1], accs[PACK * b + t][:], ALU.mult, ALU.add
                         )
-                    result = ring.tile([P, 2, part], F32, name="result", tag="window", bufs=12, align_bytes=64)
+                    result = ring.tile([P, group, part], F32, name="result", tag="window", bufs=12, align_bytes=64)
                     nc.scalar.activation(result[:], summed[:], ACT.Tanh)
-                    nc.sync.dma_start(out_rows[b, :, pair : pair + 2, cols], result[:])
+                    nc.sync.dma_start(out_rows[b, :, pair : pair + group, cols], result[:])

@@ -55,8 +55,8 @@ def tile_list_carton_seal_join_kernel(
                 lo = 32 * quad + first_row
                 queue.dma_start(plane[lo : lo + rows, :].bitcast(I32), src[:, 4 * quad : 4 * quad + 4, :].bitcast(I32))
 
-        def load_weight(src, a, b, pieces=1):
-            raw = ring.tile([P, PACK, K_PASS], F32, name="raw", tag="raw", bufs=6, align_bytes=64)
+        def load_weight(src, a, b, pieces=1, tag="raw", bufs=5):
+            raw = ring.tile([P, PACK, K_PASS], F32, name="raw", tag=tag, bufs=bufs, align_bytes=64)
             rows = src[K_PASS * a : K_PASS * (a + 1), K_PASS * b : K_PASS * (b + 1)].rearrange("(p j) c -> p j c", j=PACK)
             step = K_PASS // pieces
             for lo in range(0, K_PASS, step):
@@ -118,30 +118,24 @@ def tile_list_carton_seal_join_kernel(
         load_scale_rows(tab2_plane, tab2_scales, 0)
         w3_raw.append(load_weight(w3, 0, 1))
         l_pos3 = load_list(pos3, "l_pos3")
-        w2_raw = keep.tile([P, 2 * H], U8, name="w2_raw", align_bytes=64)
-        nc.sync.dma_start(w2_raw[:].bitcast(I32), w2_words[0].bitcast(I32))
-        load_scale_rows(w_plane, w2_scales, 0)
-        w4_raw = keep.tile([P, 2, H], I32, name="w4_raw", align_bytes=64)
-        nc.sync.dma_start(w4_raw[:], w4_words.rearrange("a p c i -> p a (c i)").bitcast(I32))
-        load_scale_rows(w_plane, w4_scales, 8)
         l_offs = load_list(offs, "l_offs")
         t1 = [load_words(tab_words[0], "t1a")]
-        w1_raw = {(a, 0): load_weight(w1, a, 0) for a in range(K // K_PASS)}
+        w1_raw = {(0, 0): load_weight(w1, 0, 0)}
         load_scale_rows(tab_plane, tab_scales, 4)
-        for a in range(K // K_PASS):
-            w1_raw[a, 1] = load_weight(w1, a, 1)
+        w1_raw[1, 0] = load_weight(w1, 1, 0)
         t1.append(load_words(tab_words[1], "t1b"))
+        load_scale_rows(w_plane, w2_scales, 0)
+        w1_raw[0, 1] = load_weight(w1, 0, 1)
+        w1_raw[1, 1] = load_weight(w1, 1, 1, tag="raw_late", bufs=1)
+        load_scale_rows(w_plane, w4_scales, 8)
+        w2_raw = keep.tile([P, 2 * H], U8, name="w2_raw", align_bytes=64)
+        nc.sync.dma_start(w2_raw[:].bitcast(I32), w2_words[0].bitcast(I32))
         l_pos2 = load_list(pos2, "l_pos2")
+        w4_raw = keep.tile([P, 2, H], I32, name="w4_raw", align_bytes=64)
+        nc.sync.dma_start(w4_raw[:], w4_words.rearrange("a p c i -> p a (c i)").bitcast(I32))
         l_pos1 = load_list(pos1, "l_pos1")
         gain = keep.tile([P, HALVES, PACK], F32, name="gain")
         nc.sync.dma_start(gain[:], gd.rearrange("(b p t) -> p b t", p=P, t=PACK))
-
-        def deal_plane(plane, dealt, b):
-            cols = slice(K_PASS * b, K_PASS * (b + 1))
-            nc.gpsimd.tensor_copy(
-                dealt[:, cols].rearrange("p (t q) -> p t q", t=PACK),
-                plane[:, cols].rearrange("p (q t) -> p t q", t=PACK),
-            )
 
         v3_plane = gather_scales(tab3_plane, l_offs3, "v3_plane")
         v3 = gather_words(t3, l_offs3, "v3")
@@ -152,35 +146,17 @@ def tile_list_carton_seal_join_kernel(
             w3_q.append(quantize(grouped, "w3_%d" % b))
         v2 = gather_words(t2, l_offs2, "v2")
         v2_plane = gather_scales(tab2_plane, l_offs2, "v2_plane")
-        w2_dealt = keep.tile([P, 2 * H], U8, name="w2_dealt", align_bytes=64)
-        for b in range(HALVES):
-            two = slice(2 * K_PASS * b, 2 * K_PASS * (b + 1))
-            nc.gpsimd.tensor_copy(
-                w2_dealt[:, two].rearrange("p (t q e) -> p t q e", t=PACK, e=2),
-                w2_raw[:, two].rearrange("p (q t e) -> p t q e", t=PACK, e=2),
-            )
         v1 = [gather_words(t1[0], l_offs, "v1a"), gather_words(t1[1], l_offs, "v1b")]
         v1_plane = gather_scales(tab_plane, l_offs, "v1_plane")
-
-        w4_dealt = keep.tile([P, 2, H], I32, name="w4_dealt", align_bytes=64)
-        w_plane_dealt = keep.tile([P, H], U8, name="w_plane_dealt", align_bytes=64)
-        for b in range(HALVES):
-            deal_plane(w_plane, w_plane_dealt, b)
-            for a in range(HALVES):
-                cols = slice(K_PASS * b, K_PASS * (b + 1))
-                nc.gpsimd.tensor_copy(
-                    w4_dealt[:, a, cols].rearrange("p (t q) -> p t q", t=PACK),
-                    w4_raw[:, a, cols].rearrange("p (q t) -> p t q", t=PACK),
-                )
 
         w1_q = {}
 
         def quantize_w1():
             width = PACK * K_PASS
             wide = [ring.tile([P, 2 * width], BF16, name="w1_wide", tag=tag, bufs=1, align_bytes=64) for tag in ("t3", "t2")]
-            place = {(0, 0): (0, 0), (1, 0): (1, 0), (0, 1): (1, 1), (1, 1): (0, 1)}
+            place = {(a, b): (b, a) for b in range(HALVES) for a in range(K // K_PASS)}
             for key, (i, u) in place.items():
-                cast_weight(w1_raw[key], wide[i][:, u * width : (u + 1) * width], False, 2)
+                cast_weight(w1_raw[key], wide[i][:, u * width : (u + 1) * width], i == 1, 4 if i == 0 else 1)
             done = [quantize(wide[i], "w1_%d" % i) for i in range(2)]
             for key, (i, u) in place.items():
                 cols = slice(u * K_PASS, (u + 1) * K_PASS)
@@ -207,7 +183,8 @@ def tile_list_carton_seal_join_kernel(
             ])
 
         def absolute(b):
-            d_abs = ring.tile([P, PACK, J], F32, name="d_abs", tag="raw", bufs=6, align_bytes=64)
+            tag, bufs = (("raw", 5), ("raw_late", 1))[b]
+            d_abs = ring.tile([P, PACK, J], F32, name="d_abs", tag=tag, bufs=bufs, align_bytes=64)
             nc.scalar.activation(d_abs[:], d_picked[b][:], ACT.Abs)
             return d_abs
 
@@ -229,16 +206,33 @@ def tile_list_carton_seal_join_kernel(
         for b in range(HALVES):
             for t in range(PACK):
                 slice_d(b, t)
+        d_abs = [absolute(0)]
         quantize_w1()
+
+        w_plane_dealt = keep.tile([P, H], U8, name="w_plane_dealt", align_bytes=64)
+        nc.vector.tensor_copy(
+            w_plane_dealt[:].rearrange("p (b t o i) -> p b o t i", b=HALVES, t=PACK, i=16),
+            w_plane[:].rearrange("p (b o i t) -> p b o t i", b=HALVES, t=PACK, i=16),
+        )
+        w2_dealt = keep.tile([P, 2 * H], U8, name="w2_dealt", align_bytes=64)
+        nc.vector.tensor_copy(
+            w2_dealt[:].bitcast(U16).rearrange("p (b t o i) -> p b o t i", b=HALVES, t=PACK, i=8),
+            w2_raw[:].bitcast(U16).rearrange("p (b o i t) -> p b o t i", b=HALVES, t=PACK, i=8),
+        )
         best = [
             keep.tile([P, PACK, J], F32, name="best0", align_bytes=64),
-            ring.tile([P, PACK, J], F32, name="best1", tag="t3", bufs=1, align_bytes=64),
+            ring.tile([P, PACK, J], F32, name="best1", tag="t2", bufs=1, align_bytes=64),
         ]
-        d_abs = []
-        for b in range(HALVES):
-            d_abs.append(absolute(b))
-            for t in range(PACK):
-                slice_b(b, t)
+        for t in range(PACK):
+            slice_b(0, t)
+        w4_dealt = keep.tile([P, 2, H], I32, name="w4_dealt", align_bytes=64)
+        nc.vector.tensor_copy(
+            w4_dealt[:].rearrange("p a (b t o i) -> p (a b) o t i", b=HALVES, t=PACK, i=4),
+            w4_raw[:].rearrange("p a (b o i t) -> p (a b) o t i", b=HALVES, t=PACK, i=4),
+        )
+        d_abs.append(absolute(1))
+        for t in range(PACK):
+            slice_b(1, t)
         z0 = join(0, [window_a(0, t) for t in range(PACK)], d_abs[0], 0, J)
         windows = [window_a(1, t) for t in range(PACK)]
         part = J // 2

from contextlib import ExitStack

import concourse.mybir as mybir

K, M, H, T, S, J = 1024, 512, 1024, 2048, 1024, 512
FLOPS = 2 * H * S * (K + M + M) + 2 * H * H * J

F32 = mybir.dt.float32
BF16 = mybir.dt.bfloat16
I32 = mybir.dt.int32
U32 = mybir.dt.uint32
U16 = mybir.dt.uint16
U8 = mybir.dt.uint8
FP8X4 = mybir.dt.float8_e4m3fn_x4
FP4X4 = mybir.dt.float4_e2m1fn_x4
ALU = mybir.AluOpType
ACT = mybir.ActivationFunctionType

P = 128
PACK = 4
K_PASS = P * PACK
N_BANK = 512
QUADS = 4
HALVES = H // K_PASS


def tile_list_carton_seal_join_kernel(
    tc, tab_words, tab_scales, tab2_words, tab2_scales, tab3_words, tab3_scales, offs, offs2, offs3,
    pos1, pos2, pos3, w1, w2_words, w2_scales, w3, w4_words, w4_scales, gd, out,
):
    nc = tc.nc
    with ExitStack() as ctx:
        keep = ctx.enter_context(tc.tile_pool(name="keep", bufs=1))
        ring = ctx.enter_context(tc.tile_pool(name="ring", bufs=1))
        psum = ctx.enter_context(tc.psum_pool(name="psum", bufs=8))

        def load_list(src, name):
            tile = keep.tile(list(src.shape), U16, name=name)
            nc.sync.dma_start(tile[:], src)
            return tile

        def load_words(src, name):
            tile = ring.tile([P, T], I32, name=name, tag=name, bufs=1, align_bytes=64)
            nc.sync.dma_start(tile[:], src.rearrange("p t i -> p (t i)").bitcast(I32))
            return tile

        def zeroed_plane(width, name, engine):
            tile = keep.tile([P, width], U8, name=name, align_bytes=64)
            engine.memset(tile[:].bitcast(I32), 0)
            return tile

        def load_scale_rows(plane, src, first_row, queue=nc.sync):
            rows = 4 * src.shape[0]
            for quad in range(QUADS):
                lo = 32 * quad + first_row
                queue.dma_start(plane[lo : lo + rows, :].bitcast(I32), src[:, 4 * quad : 4 * quad + 4, :].bitcast(I32))

        def load_weight(src, a, b, pieces=1, tag="raw", bufs=5):
            raw = ring.tile([P, PACK, K_PASS], F32, name="raw", tag=tag, bufs=bufs, align_bytes=64)
            rows = src[K_PASS * a : K_PASS * (a + 1), K_PASS * b : K_PASS * (b + 1)].rearrange("(p j) c -> p j c", j=PACK)
            step = K_PASS // pieces
            for lo in range(0, K_PASS, step):
                nc.sync.dma_start(raw[:, :, lo : lo + step], rows[:, :, lo : lo + step])
            return raw

        def gather_words(table, offsets, name):
            picked = keep.tile([P, S], U32, name=name, align_bytes=64)
            nc.vector.tensor_copy(picked[:], table[:].bitcast(U32).indirect(offsets[:]))
            return picked

        def gather_scales(plane, offsets, name):
            picked = keep.tile([P, S], U8, name=name, align_bytes=64)
            nc.vector.tensor_copy(picked[:], plane[:].indirect(offsets[:]))
            return picked

        def cast_weight(raw, grouped, on_scalar, pieces=1):
            dst = grouped.rearrange("p (t q j) -> p q t j", t=PACK, j=PACK)
            src = raw[:].rearrange("p j (q t) -> p q t j", t=PACK)
            step = P // pieces
            for lo in range(0, P, step):
                if on_scalar:
                    nc.scalar.copy(dst[:, lo : lo + step], src[:, lo : lo + step])
                else:
                    nc.gpsimd.tensor_scalar(dst[:, lo : lo + step], src[:, lo : lo + step], 1.0, 0.0, ALU.mult, ALU.add)

        def quantize(grouped, name):
            width = grouped.shape[1] // PACK
            codes = keep.tile([P, width], U32, name=name + "_codes", align_bytes=64)
            scales = keep.tile([P, width], U8, name=name + "_scales", align_bytes=64)
            nc.vector.quantize_mx(out=codes[:].bitcast(FP8X4), scales=scales[:], in_=grouped[:])
            return codes, scales

        def first_stage(passes):
            window = ring.tile([P, S], F32, name="window", tag="window", bufs=12, align_bytes=64)
            for h in range(S // N_BANK):
                cols = slice(h * N_BANK, (h + 1) * N_BANK)
                acc = psum.tile([P, N_BANK], F32, name="acc", tag="acc")
                for i, (lhs, lhs_scale, words, plane, row) in enumerate(passes):
                    nc.tensor.matmul_mx(
                        out=acc[:], lhsT=lhs, lhsT_scale=lhs_scale,
                        rhs=words[:, cols].bitcast(FP8X4), rhs_scale=plane[row:P, cols],
                        start=(i == 0), stop=(i == len(passes) - 1),
                    )
                nc.scalar.copy(window[:, cols], acc[:])
            return window

        tab3_plane = zeroed_plane(T, "tab3_plane", nc.gpsimd)
        tab2_plane = zeroed_plane(T, "tab2_plane", nc.vector)
        w_plane = zeroed_plane(H, "w_plane", nc.vector)
        tab_plane = zeroed_plane(T, "tab_plane", nc.vector)

        l_offs3 = load_list(offs3, "l_offs3")
        t3 = load_words(tab3_words[0], "t3")
        load_scale_rows(tab3_plane, tab3_scales, 12, nc.scalar)
        w3_raw = [load_weight(w3, 0, 0, 2)]
        l_offs2 = load_list(offs2, "l_offs2")
        t2 = load_words(tab2_words[0], "t2")
        load_scale_rows(tab2_plane, tab2_scales, 0)
        w3_raw.append(load_weight(w3, 0, 1))
        l_pos3 = load_list(pos3, "l_pos3")
        l_offs = load_list(offs, "l_offs")
        t1 = [load_words(tab_words[0], "t1a")]
        w1_raw = {(0, 0): load_weight(w1, 0, 0)}
        load_scale_rows(tab_plane, tab_scales, 4)
        w1_raw[1, 0] = load_weight(w1, 1, 0)
        t1.append(load_words(tab_words[1], "t1b"))
        load_scale_rows(w_plane, w2_scales, 0)
        w1_raw[0, 1] = load_weight(w1, 0, 1)
        w1_raw[1, 1] = load_weight(w1, 1, 1, tag="raw_late", bufs=1)
        load_scale_rows(w_plane, w4_scales, 8)
        w2_raw = keep.tile([P, 2 * H], U8, name="w2_raw", align_bytes=64)
        nc.sync.dma_start(w2_raw[:].bitcast(I32), w2_words[0].bitcast(I32))
        l_pos2 = load_list(pos2, "l_pos2")
        w4_raw = keep.tile([P, 2, H], I32, name="w4_raw", align_bytes=64)
        nc.sync.dma_start(w4_raw[:], w4_words.rearrange("a p c i -> p a (c i)").bitcast(I32))
        l_pos1 = load_list(pos1, "l_pos1")
        gain = keep.tile([P, HALVES, PACK], F32, name="gain")
        nc.sync.dma_start(gain[:], gd.rearrange("(b p t) -> p b t", p=P, t=PACK))

        v3_plane = gather_scales(tab3_plane, l_offs3, "v3_plane")
        v3 = gather_words(t3, l_offs3, "v3")
        w3_q = []
        for b in range(HALVES):
            grouped = ring.tile([P, PACK * K_PASS], BF16, name="grouped", tag="grouped", bufs=2, align_bytes=64)
            cast_weight(w3_raw[b], grouped[:], True, 2 - b)
            w3_q.append(quantize(grouped, "w3_%d" % b))
        v2 = gather_words(t2, l_offs2, "v2")
        v2_plane = gather_scales(tab2_plane, l_offs2, "v2_plane")
        v1 = [gather_words(t1[0], l_offs, "v1a"), gather_words(t1[1], l_offs, "v1b")]
        v1_plane = gather_scales(tab_plane, l_offs, "v1_plane")

        w1_q = {}

        def quantize_w1():
            width = PACK * K_PASS
            wide = [ring.tile([P, 2 * width], BF16, name="w1_wide", tag=tag, bufs=1, align_bytes=64) for tag in ("t3", "t2")]
            place = {(a, b): (b, a) for b in range(HALVES) for a in range(K // K_PASS)}
            for key, (i, u) in place.items():
                cast_weight(w1_raw[key], wide[i][:, u * width : (u + 1) * width], i == 1, 4 if i == 0 else 1)
            done = [quantize(wide[i], "w1_%d" % i) for i in range(2)]
            for key, (i, u) in place.items():
                cols = slice(u * K_PASS, (u + 1) * K_PASS)
                w1_q[key] = (done[i][0][:, cols], done[i][1][:, cols])

        d_picked = [keep.tile([P, PACK, J], F32, name="d_picked%d" % b, align_bytes=64) for b in range(HALVES)]

        def slice_d(b, t):
            cols = slice(P * t, P * (t + 1))
            codes, scales = w3_q[b]
            window = first_stage([(codes[:, cols].bitcast(FP8X4), scales[:, cols], v3, v3_plane, 12)])
            nc.vector.tensor_copy(d_picked[b][:, t, :], window[:].indirect(l_pos3[:]))

        def slice_b(b, t):
            lo = K_PASS * b + P * t
            window = first_stage([(w2_dealt[:, 2 * lo : 2 * (lo + P)].bitcast(FP4X4), w_plane_dealt[:, lo : lo + P], v2, v2_plane, 0)])
            nc.vector.tensor_tensor(best[b][:, t, :], window[:].indirect(l_pos2[:]), d_abs[b][:, t, :], ALU.subtract)

        def window_a(b, t):
            cols = slice(P * t, P * (t + 1))
            return first_stage([
                (w1_q[a, b][0][:, cols].bitcast(FP8X4), w1_q[a, b][1][:, cols], v1[a], v1_plane, 4 + 4 * a)
                for a in range(K // K_PASS)
            ])

        def absolute(b):
            tag, bufs = (("raw", 5), ("raw_late", 1))[b]
            d_abs = ring.tile([P, PACK, J], F32, name="d_abs", tag=tag, bufs=bufs, align_bytes=64)
            nc.scalar.activation(d_abs[:], d_picked[b][:], ACT.Abs)
            return d_abs

        def join(b, windows, d_abs, lo, width):
            cols = slice(lo, lo + width)
            a_picked = ring.tile([P, PACK, width], F32, name="a_picked", tag="t1a", bufs=1, align_bytes=64)
            for t in range(PACK):
                picked = windows[t][:].indirect(l_pos1[:, lo // 16 : (lo + width) // 16])
                nc.vector.tensor_tensor(a_picked[:, t, :], picked, d_abs[:, t, cols], ALU.subtract)
            grouped = ring.tile([P, PACK * width], BF16, name="grouped", tag="grouped", bufs=2, align_bytes=64)
            nc.vector.tensor_tensor(
                grouped[:].rearrange("p (c i t) -> p c t i", i=4, t=PACK),
                a_picked[:].rearrange("p t (c i) -> p c t i", i=4),
                best[b][:, :, cols].rearrange("p t (c i) -> p c t i", i=4),
                ALU.max,
            )
            return quantize(grouped, "z%d_%d" % (b, lo))

        for b in range(HALVES):
            for t in range(PACK):
                slice_d(b, t)
        d_abs = [absolute(0)]
        quantize_w1()

        w_plane_dealt = keep.tile([P, H], U8, name="w_plane_dealt", align_bytes=64)
        nc.vector.tensor_copy(
            w_plane_dealt[:].rearrange("p (b t o i) -> p b o t i", b=HALVES, t=PACK, i=16),
            w_plane[:].rearrange("p (b o i t) -> p b o t i", b=HALVES, t=PACK, i=16),
        )
        w2_dealt = keep.tile([P, 2 * H], U8, name="w2_dealt", align_bytes=64)
        nc.vector.tensor_copy(
            w2_dealt[:].bitcast(U16).rearrange("p (b t o i) -> p b o t i", b=HALVES, t=PACK, i=8),
            w2_raw[:].bitcast(U16).rearrange("p (b o i t) -> p b o t i", b=HALVES, t=PACK, i=8),
        )
        best = [
            keep.tile([P, PACK, J], F32, name="best0", align_bytes=64),
            ring.tile([P, PACK, J], F32, name="best1", tag="t2", bufs=1, align_bytes=64),
        ]
        for t in range(PACK):
            slice_b(0, t)
        w4_dealt = keep.tile([P, 2, H], I32, name="w4_dealt", align_bytes=64)
        nc.vector.tensor_copy(
            w4_dealt[:].rearrange("p a (b t o i) -> p (a b) o t i", b=HALVES, t=PACK, i=4),
            w4_raw[:].rearrange("p a (b o i t) -> p (a b) o t i", b=HALVES, t=PACK, i=4),
        )
        d_abs.append(absolute(1))
        for t in range(PACK):
            slice_b(1, t)
        z0 = join(0, [window_a(0, t) for t in range(PACK)], d_abs[0], 0, J)
        windows = [window_a(1, t) for t in range(PACK)]
        part = J // 2
        z1 = [join(1, windows, d_abs[1], lo, part) for lo in range(0, J, part)]

        out_rows = out.rearrange("(b p t) j -> b p t j", p=P, t=PACK)
        for h in range(J // part):
            cols = slice(h * part, (h + 1) * part)
            moving = [(z0[0][:, cols], z0[1][:, cols]), (z1[h][0][:], z1[h][1][:])]
            group = 2 if h == 0 else 1
            accs = [psum.tile([P, part], F32, name="acc", tag="acc") for n in range(H // P)]

            def y_pass(n, a):
                nc.tensor.matmul_mx(
                    out=accs[n][:], lhsT=w4_dealt[:, a, P * n : P * (n + 1)].bitcast(FP8X4),
                    lhsT_scale=w_plane_dealt[8 + 4 * a : P, P * n : P * (n + 1)],
                    rhs=moving[a][0].bitcast(FP8X4), rhs_scale=moving[a][1],
                    start=(a == 0), stop=(a == HALVES - 1),
                )

            if h == 0:
                for n in range(H // P):
                    y_pass(n, 0)
            for b in range(HALVES):
                for pair in range(0, PACK, group):
                    summed = ring.tile([P, group, part], F32, name="summed", tag="summed", bufs=4, align_bytes=64)
                    for u in range(group):
                        t = pair + u
                        if h > 0:
                            y_pass(PACK * b + t, 0)
                        y_pass(PACK * b + t, 1)
                        nc.vector.scalar_tensor_tensor(
                            summed[:, u, :], d_picked[b][:, t, cols], gain[:, b, t : t + 1], accs[PACK * b + t][:], ALU.mult, ALU.add
                        )
                    result = ring.tile([P, group, part], F32, name="result", tag="window", bufs=12, align_bytes=64)
                    nc.scalar.activation(result[:], summed[:], ACT.Tanh)
                    nc.sync.dma_start(out_rows[b, :, pair : pair + group, cols], result[:])
